import numpy as np
import ml_dtypes


def mxq(x, axis, fmt="e4m3"):
    dtype, down = {"e4m3": (ml_dtypes.float8_e4m3fn, 7), "e5m2": (ml_dtypes.float8_e5m2, 14)}[fmt]
    v = np.moveaxis(np.asarray(x, np.float32).astype(ml_dtypes.bfloat16).astype(np.float64), axis, -1)
    blocks = v.reshape(v.shape[:-1] + (-1, 32))
    amax = np.abs(blocks).max(-1, keepdims=True)
    byte = np.maximum(np.where(amax > 0, np.frexp(amax)[1] - 1 + 127, 0) - down, 1)
    scale = np.exp2(byte - 127.0)
    codes = (blocks / scale).astype(np.float32).astype(dtype).astype(np.float64)
    return np.moveaxis((codes * scale).reshape(v.shape), -1, axis)


WIDE = False


def mx_kscale(k):
    if not WIDE:
        return np.ones(k)
    levels = np.array([10, -10, 5, -5, 0])
    if k % 512:
        return np.exp2(np.random.permutation(np.resize(levels, k // 32))).repeat(32)
    a = np.empty((k // 512, 16))
    for p in range(k // 512):
        a[p, :8] = np.random.permutation(np.resize(levels, 8))
        for g in range(8):
            far = levels[np.abs(levels - a[p, g]) >= 10]
            a[p, g + 8] = far[np.random.randint(len(far))]
    return np.exp2(a.ravel()).repeat(32)


def f64(x):
    return np.asarray(x).astype(np.float64)


def striped(idx):
    return np.tile(idx.reshape(-1, 16).T, (8, 1)).astype(np.uint16)


def unstriped(offs):
    return offs[:16].T.reshape(-1).astype(np.int64)


E2M1 = np.array([0.0, 0.5, 1.0, 1.5, 2.0, 3.0, 4.0, 6.0, -0.0, -0.5, -1.0, -1.5, -2.0, -3.0, -4.0, -6.0])


def pack_weight(w, fmt):
    k, n = w.shape
    w = f64(np.asarray(w, np.float32).astype(ml_dtypes.bfloat16)).reshape(k // 32, 32, n)
    amax = np.abs(w).max(1)
    if fmt == "e4m3":
        byte = np.frexp(amax)[1] - 1 + 127 - 7
    else:
        mant, ex = np.frexp(amax / 6.0)
        byte = np.where(mant > 0.5, ex, ex - 1) + 127
    byte = np.clip(np.where(amax > 0, byte, 1), 1, 254)
    scaled = (w * np.exp2(127.0 - byte)[:, None, :]).reshape(k, n).astype(np.float32)
    by_word = np.ascontiguousarray(scaled.reshape(k // 512, 128, 4, n).transpose(0, 1, 3, 2))
    if fmt == "e4m3":
        words = by_word.astype(ml_dtypes.float8_e4m3fn).view(np.uint8)
    else:
        c = by_word.astype(ml_dtypes.float4_e2m1fn).view(np.uint8) & 0xF
        words = (c[..., 0::2] | (c[..., 1::2] << 4)).reshape(k // 512, 128, 2 * n)
    return np.ascontiguousarray(words), np.ascontiguousarray(byte.astype(np.uint8).reshape(k // 512, 16, n))


def unpack_weight(words, scales, fmt):
    g, _, n = scales.shape
    words = np.ascontiguousarray(words).reshape(g, 128, n, -1)
    if fmt == "e4m3":
        vals = words.view(ml_dtypes.float8_e4m3fn).astype(np.float64)
    else:
        nib = np.empty((g, 128, n, 4), np.uint8)
        nib[..., 0::2] = words & 0xF
        nib[..., 1::2] = words >> 4
        vals = E2M1[nib]
    vals = vals * np.repeat(np.exp2(scales.astype(np.float64) - 127.0), 8, axis=1)[..., None]
    return vals.transpose(0, 1, 3, 2).reshape(g * 512, n)


def gelu(v):
    return 0.5 * v * (1.0 + np.tanh(np.sqrt(2.0 / np.pi) * (v + 0.044715 * v**3)))


def bf(x):
    return np.asarray(x, np.float32).astype(ml_dtypes.bfloat16)


def planes(Y):
    n, m = Y.shape
    b = f64(bf(Y)).reshape(n // 32, 32, m)
    amax = np.abs(b).max(1)
    byte = np.clip(np.where(amax > 0, np.frexp(amax)[1] - 1 + 127 - 7, 1), 1, 254)
    codes = (b * np.exp2(127.0 - byte)[:, None, :]).reshape(n, m).astype(np.float32).astype(ml_dtypes.float8_e4m3fn).view(np.uint8)
    words = codes.reshape(n // 512, 128, 4, m).transpose(0, 1, 3, 2)
    return np.ascontiguousarray(words), np.ascontiguousarray(byte.astype(np.uint8).reshape(n // 512, 16, m))


K, T, S, H, T2, P, N = 1024, 2048, 1024, 512, 2048, 1024, 1024

def setup_inputs():
    n = np.random.standard_normal
    s = mx_kscale(K)[:, None]
    u = mx_kscale(H)[:, None]
    tab_words, tab_scales = pack_weight(n((K, T)) * s, "e4m3")
    w2_words, w2_scales = pack_weight(0.8 * n((H, H)) / np.sqrt(H) / u, "e2m1")
    w1 = 0.85 * n((K, H)) / np.sqrt(K) / s
    w3 = n((H, N)) / np.sqrt(H) * np.exp(0.8 * n(N))[None, :] / u
    return {
        "tab_words": tab_words, "tab_scales": tab_scales,
        "offs": striped(np.random.permutation(T)[:S]),
        "offs2": striped(np.random.permutation(T2)[:S]),
        "offs3": striped(np.random.permutation(T2)[:P]),
        "w1": w1.astype(np.float32),
        "gain": (np.random.uniform(0.6, 1.6, H) * u[:, 0]).astype(np.float32),
        "w2_words": w2_words, "w2_scales": w2_scales,
        "page0": (0.8 * n((H, T2))).astype(np.float32),
        "wgs": np.exp(0.3 * n((128, S))).astype(np.float32),
        "vthr": n(H).astype(np.float32),
        "base": np.random.uniform(0.3, 0.7, H).astype(np.float32),
        "view": (2.0 * n((H, P)) * u).astype(np.float32),
        "w3": w3.astype(np.float32),
    }

def reference(tab_words, tab_scales, offs, offs2, offs3, w1, gain, w2_words, w2_scales, page0, wgs, vthr, base, view, w3):
    v = unpack_weight(tab_words, tab_scales, "e4m3")[:, unstriped(offs)]
    z = mxq(f64(w1), 0, "e4m3").T @ v
    f = f64(gain)[:, None] * np.tanh(z)
    w2 = unpack_weight(w2_words, w2_scales, "e2m1")
    h = z + (w2.T @ mxq(f, 0, "e4m3"))
    page = f64(page0).copy()
    page[:, unstriped(offs2)] = np.tile(f64(wgs), (H // 128, 1)) * h
    a = 1.0 / (1.0 + np.exp(-(page[:, unstriped(offs3)] + f64(vthr)[:, None])))
    d = (a - f64(base)[:, None]) * f64(view)
    y = mxq(f64(w3), 0, "e4m3").T @ mxq(d, 0, "e4m3")
    words, scales = planes(y)
    return y, words, scales

@@ -1,0 +1,487 @@
+from contextlib import ExitStack
+
+import concourse.mybir as mybir
+
+K, T, S, H, T2, PW, N = 1024, 2048, 1024, 512, 2048, 1024, 1024
+FLOPS = 2 * K * H * S + 2 * H * H * S + 2 * H * N * PW
+
+F32 = mybir.dt.float32
+BF16 = mybir.dt.bfloat16
+I32 = mybir.dt.int32
+U32 = mybir.dt.uint32
+U16 = mybir.dt.uint16
+U8 = mybir.dt.uint8
+E4M3 = mybir.dt.float8_e4m3fn_x4
+E2M1 = mybir.dt.float4_e2m1fn_x4
+ACT = mybir.ActivationFunctionType
+ALU = mybir.AluOpType
+
+P = 128
+BANK = 512
+PIECE = 256
+
+
+def entries(offsets, start, count):
+    return offsets[:, start // 16 : (start + count) // 16]
+
+
+def tile_list_wiki_revision_patrol_kernel(
+    tc, tab_words, tab_scales, offs, offs2, offs3, w1, gain, w2_words, w2_scales, page0, wgs, vthr, base, view, w3,
+    out_0, out_1, out_2,
+):
+    nc = tc.nc
+    with ExitStack() as ctx:
+        keep = ctx.enter_context(tc.tile_pool(name="keep", bufs=1))
+        ring = ctx.enter_context(tc.tile_pool(name="ring", bufs=2))
+        psum = ctx.enter_context(tc.psum_pool(name="psum", bufs=4))
+
+        def held(shape, dtype, name):
+            return keep.tile(shape, dtype, name=name, align_bytes=64)
+
+        def shared(shape, dtype, tag, bufs):
+            return ring.tile(shape, dtype, name=tag, tag=tag, bufs=bufs, align_bytes=64)
+
+        def bank(tag):
+            return psum.tile([P, BANK], F32, name=tag, tag=tag)
+
+        idx1 = keep.tile([P, S // 16], U16, name="idx1")
+        idx2 = keep.tile([P, S // 16], U16, name="idx2")
+        idx3 = keep.tile([P, PW // 16], U16, name="idx3")
+
+        nc.sync.dma_start(idx1[:], offs)
+        w2_raw = held([P, 2 * H], U8, "w2_raw")
+        nc.sync.dma_start(out=w2_raw[:].bitcast(I32), in_=w2_words[0].bitcast(I32))
+        tab_w = [held([P, T], U32, "tab_w%d" % a) for a in range(2)]
+        w1_raw = [shared([P, 4, H], F32, "slab%d" % a, 1) for a in range(2)]
+
+        def load_words(a):
+            nc.sync.dma_start(out=tab_w[a][:].bitcast(I32), in_=tab_words[a].rearrange("p n i -> p (n i)").bitcast(I32))
+
+        load_words(0)
+        for a in range(2):
+            nc.sync.dma_start(out=w1_raw[a][:], in_=w1[512 * a : 512 * (a + 1), :].rearrange("(p i) r -> p i r", i=4))
+        load_words(1)
+
+        tab_s = held([P, T], U8, "tab_s")
+        w2_sraw = held([P, H], U8, "w2_sraw")
+        gain_t = held([P, 4], F32, "gain_t")
+        vthr_t = held([P, 4], F32, "vthr_t")
+        base_t = held([P, 4], F32, "base_t")
+        nc.gpsimd.memset(tab_s[:].bitcast(I32), 0)
+        nc.gpsimd.memset(w2_sraw[:].bitcast(I32), 0)
+        for q in range(4):
+            nc.gpsimd.dma_start(
+                out=tab_s[32 * q : 32 * q + 8, :].bitcast(I32), in_=tab_scales[:, 4 * q : 4 * q + 4, :].bitcast(I32)
+            )
+        for q in range(4):
+            nc.gpsimd.dma_start(
+                out=w2_sraw[32 * q : 32 * q + 4, :].bitcast(I32), in_=w2_scales[0, 4 * q : 4 * q + 4, :].bitcast(I32)
+            )
+        nc.gpsimd.dma_start(out=gain_t[:], in_=gain.rearrange("(p t) -> p t", t=4))
+        nc.gpsimd.dma_start(out=vthr_t[:], in_=vthr.rearrange("(p t) -> p t", t=4))
+        nc.gpsimd.dma_start(out=base_t[:], in_=base.rearrange("(p t) -> p t", t=4))
+
+        nc.sync.dma_start(idx2[:], offs2)
+        wgs_rows = wgs.rearrange("(q t) j -> q t j", t=4)
+        page_rows = page0.rearrange("(p t) c -> p t c", t=4)
+        view_rows = view.rearrange("(p t) j -> p t j", t=4)
+
+        def load_wgs(tile, t0, count, start):
+            for q in (0, 2, 1, 3):
+                nc.sync.dma_start(
+                    out=tile[32 * q : 32 * q + 32, :, :], in_=wgs_rows[:, t0 : t0 + count, start : start + 512]
+                )
+
+        page = [held([P, T2], F32, "page%d" % t) for t in range(4)]
+        wg_first = [shared([P, 2, 512], F32, "quad", 4) for pair in range(2)]
+        wg_second = shared([P, 4, 512], F32, "wide0", 1)
+        for pair in range(2):
+            load_wgs(wg_first[pair], 2 * pair, 2, 0)
+            for t in (2 * pair, 2 * pair + 1):
+                nc.sync.dma_start(out=page[t][:], in_=page_rows[:, t, :])
+        load_wgs(wg_second, 0, 4, 512)
+        nc.sync.dma_start(idx3[:], offs3)
+
+        def wgs_for(c, t):
+            lo = PIECE * (c % 2)
+            if c < 2:
+                return wg_first[t // 2][:, t % 2, lo : lo + PIECE]
+            return wg_second[:, t, lo : lo + PIECE]
+
+        w2_c = held([P, 2 * H], U8, "w2_c")
+        w2_s = held([P, H], U8, "w2_s")
+        nc.vector.tensor_copy(
+            out=w2_c[:].rearrange("p (t q b) -> p q t b", t=4, b=2), in_=w2_raw[:].rearrange("p (q t b) -> p q t b", t=4, b=2)
+        )
+        got_w0 = held([P, S], U32, "got_w0")
+        nc.vector.tensor_copy(got_w0[:], tab_w[0][:].indirect(idx1[:]))
+        got_s_first = held([P, PIECE], U8, "got_s_first")
+        got_s_rest = held([P, S - PIECE], U8, "got_s_rest")
+        nc.vector.tensor_copy(got_s_first[:], tab_s[:].indirect(entries(idx1, 0, PIECE)))
+        nc.vector.tensor_copy(got_s_rest[:], tab_s[:].indirect(entries(idx1, PIECE, S - PIECE)))
+
+        def deal_columns(engine_copy, grouped, raw, lo, hi):
+            engine_copy(
+                out=grouped[:].rearrange("p (t m i) -> p m i t", t=4, i=4)[:, lo:hi],
+                in_=raw[:].rearrange("p i (m t) -> p m i t", t=4)[:, lo:hi],
+            )
+
+        w1_c = [held([P, H], U32, "w1_c%d" % a) for a in range(2)]
+        w1_s = [held([P, H], U8, "w1_s%d" % a) for a in range(2)]
+        w1_b = [shared([P, 4 * H], BF16, "wb", 2) for a in range(2)]
+        deal_columns(nc.scalar.copy, w1_b[0], w1_raw[0], 0, 128)
+        nc.vector.quantize_mx(out=w1_c[0][:].bitcast(E4M3), scales=w1_s[0][:], in_=w1_b[0][:])
+        deal_columns(nc.scalar.copy, w1_b[1], w1_raw[1], 0, 64)
+        deal_columns(nc.vector.tensor_copy, w1_b[1], w1_raw[1], 64, 128)
+        nc.vector.quantize_mx(out=w1_c[1][:].bitcast(E4M3), scales=w1_s[1][:], in_=w1_b[1][:])
+
+        got_w1 = {}
+
+        def gather_words(first, count, tile):
+            nc.vector.tensor_copy(tile[:], tab_w[1][:].indirect(entries(idx1, PIECE * first, PIECE * count)))
+            for k in range(count):
+                got_w1[first + k] = tile[:, PIECE * k : PIECE * (k + 1)]
+
+        def first_product(out, t, a, c, lo, width, start, stop):
+            j0 = PIECE * c + lo
+            moving = got_w0[:, j0 : j0 + width] if a == 0 else got_w1[c][:, lo : lo + width]
+            if c == 0:
+                scales = got_s_first[4 * a : P, j0 : j0 + width]
+            else:
+                scales = got_s_rest[4 * a : P, j0 - PIECE : j0 - PIECE + width]
+            nc.tensor.matmul_mx(
+                out=out,
+                lhsT=w1_c[a][:, P * t : P * (t + 1)].bitcast(E4M3),
+                lhsT_scale=w1_s[a][:, P * t : P * (t + 1)],
+                rhs=moving.bitcast(E4M3),
+                rhs_scale=scales,
+                start=start,
+                stop=stop,
+            )
+
+        def second_product(out, t, codes, scales, start, stop):
+            nc.tensor.matmul_mx(
+                out=out,
+                lhsT=w2_c[:, 2 * P * t : 2 * P * (t + 1)].bitcast(E2M1),
+                lhsT_scale=w2_s[:, P * t : P * (t + 1)],
+                rhs=codes.bitcast(E4M3),
+                rhs_scale=scales,
+                start=start,
+                stop=stop,
+            )
+
+        def interleave(engine_copy, grouped, rows):
+            engine_copy(
+                out=grouped.rearrange("p (c i t) -> p c t i", i=4, t=4),
+                in_=rows.rearrange("p t (c i) -> p c t i", i=4),
+            )
+
+        gather_words(0, 1, held([P, PIECE], U32, "got_w1_0"))
+        gather_words(1, 1, held([P, PIECE], U32, "got_w1_1"))
+        nc.vector.tensor_copy(
+            out=w2_s[:].rearrange("p (t q) -> p q t", t=4), in_=w2_sraw[:].rearrange("p (q t) -> p q t", t=4)
+        )
+        z_banks = [bank("z"), bank("z")]
+        for a in range(2):
+            for half in range(2):
+                for t in range(4):
+                    first_product(
+                        z_banks[half][:, P * t : P * (t + 1)], t, a, 0, P * half, P,
+                        start=(a == 0 and t == 0), stop=(a == 1 and t == 3),
+                    )
+        bent = []
+        for half in range(2):
+            th = shared([P, BANK], F32, "th", 3)
+            nc.scalar.activation(
+                out=th[:].rearrange("p (j t) -> p j t", t=4),
+                in_=z_banks[half][:].rearrange("p (t j) -> p j t", t=4),
+                func=ACT.Tanh,
+            )
+            bent.append(th)
+        z_sb = {}
+        z_sb[0, 1] = held([P, 2, PIECE], F32, "z_01")
+        for half in range(2):
+            nc.scalar.copy(
+                out=z_sb[0, 1][:, :, P * half : P * (half + 1)],
+                in_=z_banks[half][:, 2 * P : 4 * P].rearrange("p (t j) -> p t j", t=2),
+            )
+        f_half = [held([P, 4 * P], BF16, "f_half%d" % half) for half in range(2)]
+        f_c0 = [held([P, P], U32, "f_c0_%d" % half) for half in range(2)]
+        f_s0 = [held([P, P], U8, "f_s0_%d" % half) for half in range(2)]
+        for half in range(2):
+            nc.vector.tensor_tensor(
+                out=f_half[half][:].rearrange("p (j t) -> p j t", t=4),
+                in0=bent[half][:].rearrange("p (j t) -> p j t", t=4),
+                in1=gain_t[:].unsqueeze(1).to_broadcast([P, P, 4]),
+                op=ALU.mult,
+            )
+        for half in range(2):
+            nc.vector.quantize_mx(out=f_c0[half][:].bitcast(E4M3), scales=f_s0[half][:], in_=f_half[half][:])
+
+        mixed = {}
+        h_pair = {}
+
+        def mix(c, operands):
+            for pair in range(2):
+                pb = bank("mix")
+                summed = c < 2 and pair == 0
+                if summed:
+                    for u in range(2):
+                        for a in range(2):
+                            first_product(
+                                pb[:, PIECE * u : PIECE * (u + 1)], u, a, c, 0, PIECE, start=(u == 0 and a == 0), stop=False
+                            )
+                for k, (codes, scales, lo, width) in enumerate(operands):
+                    for u in range(2):
+                        col = PIECE * u + lo
+                        last = k == len(operands) - 1 and u == 1
+                        second_product(
+                            pb[:, col : col + width], 2 * pair + u, codes, scales,
+                            start=not summed, stop=last or not summed,
+                        )
+                if summed:
+                    h_pair[c] = shared([P, BANK], F32, ("after1", "h_pair1")[c], 1)
+                    nc.scalar.copy(out=h_pair[c][:], in_=pb[:])
+                else:
+                    mixed[c, pair] = pb
+
+        mix(0, [(f_c0[half][:], f_s0[half][:], P * half, P) for half in range(2)])
+
+        def prepare(c):
+            f_rows = shared([P, 4, PIECE], BF16, "f_rows", 2)
+            for pair in range(2):
+                zb = bank("z")
+                for u in range(2):
+                    for a in range(2):
+                        first_product(
+                            zb[:, PIECE * u : PIECE * (u + 1)], 2 * pair + u, a, c, 0, PIECE, start=(a == 0), stop=(a == 1)
+                        )
+                th = shared([P, BANK], F32, "th", 3)
+                nc.scalar.activation(out=th[:], in_=zb[:], func=ACT.Tanh)
+                if c >= 2 or pair == 1:
+                    z_sb[c, pair] = held([P, 2, PIECE], F32, "z_%d%d" % (c, pair))
+                    nc.scalar.copy(out=z_sb[c, pair][:].rearrange("p t j -> p (t j)"), in_=zb[:])
+                for u in range(2):
+                    t = 2 * pair + u
+                    nc.scalar.activation(
+                        out=f_rows[:, t, :], in_=th[:, PIECE * u : PIECE * (u + 1)], func=ACT.Copy, scale=gain_t[:, t : t + 1]
+                    )
+            f_b = shared([P, 4 * PIECE], BF16, "hold%d" % c, 1)
+            interleave(nc.scalar.copy, f_b[:], f_rows[:])
+            return f_b
+
+        def quantise_f(c, f_b):
+            f_c = shared([P, PIECE], U32, "after%d" % c, 1)
+            f_s = held([P, PIECE], U8, "f_s%d" % c)
+            nc.vector.quantize_mx(out=f_c[:].bitcast(E4M3), scales=f_s[:], in_=f_b[:])
+            mix(c, [(f_c[:], f_s[:], 0, PIECE)])
+
+        h_rows = {}
+
+        def add_z(c, t, tag="h", bufs=3):
+            h = shared([P, PIECE], F32, tag, bufs)
+            u = t % 2
+            nc.vector.tensor_tensor(
+                out=h[:], in0=mixed[c, t // 2][:, PIECE * u : PIECE * (u + 1)], in1=z_sb[c, t // 2][:, u, :], op=ALU.add
+            )
+            h_rows[c, t] = h[:]
+
+        def put(c, t):
+            if c < 2 and t < 2:
+                h = h_pair[c][:, PIECE * t : PIECE * (t + 1)]
+            else:
+                h = h_rows[c, t]
+            nc.vector.tensor_tensor(page[t][:].indirect(entries(idx2, PIECE * c, PIECE)), h, wgs_for(c, t), ALU.mult)
+
+        def look(t, start, count, tag):
+            seen = shared([P, count], F32, tag, 1)
+            nc.scalar.activation(
+                out=seen[:], in_=page[t][:].indirect(entries(idx3, start, count)), func=ACT.Sigmoid, bias=vthr_t[:, t : t + 1]
+            )
+            return seen
+
+        d_rows = [held([P, 4, 512], BF16, "d_rows%d" % half) for half in range(2)]
+        view_t = [shared([P, PW], F32, "view%d" % t, 1) for t in range(4)]
+
+        def weigh(t, seen, seen_start, start, count):
+            half, lo = divmod(start, 512)
+            nc.vector.scalar_tensor_tensor(
+                out=d_rows[half][:, t, lo : lo + count],
+                in0=seen[:, start - seen_start : start - seen_start + count],
+                scalar=base_t[:, t : t + 1],
+                in1=view_t[t][:, start : start + count],
+                op0=ALU.subtract,
+                op1=ALU.mult,
+            )
+
+        def weigh_all(t, seen):
+            for half in range(2):
+                weigh(t, seen, 0, 512 * half, 512)
+
+        f_b1 = prepare(1)
+        put(0, 0)
+        put(0, 1)
+        quantise_f(1, f_b1)
+        gather_words(2, 2, shared([P, 2 * PIECE], U32, "hold1", 1))
+        f_b2 = prepare(2)
+        f_b3 = prepare(3)
+
+        w3_b = []
+        for g in range(2):
+            raw = shared([P, 4, 512], F32, "slab%d" % g, 1)
+            nc.sync.dma_start(out=raw[:], in_=w3.rearrange("(p i) n -> p i n", i=4)[:, :, 512 * g : 512 * (g + 1)])
+            grouped = shared([P, 4 * 512], BF16, "wb", 2)
+            deal_columns(nc.scalar.copy, grouped, raw, 0, 128)
+            w3_b.append(grouped)
+        for t in range(4):
+            nc.sync.dma_start(out=view_t[t][:], in_=view_rows[:, t, :])
+
+        put(1, 0)
+        add_z(0, 2, "after2", 1)
+        put(1, 1)
+        add_z(0, 3)
+        put(0, 2)
+        quantise_f(2, f_b2)
+        add_z(1, 2, "hold2", 1)
+        put(0, 3)
+        add_z(1, 3, "after3", 1)
+        put(1, 2)
+        add_z(2, 0)
+        put(1, 3)
+        quantise_f(3, f_b3)
+        add_z(2, 1, "hold3", 1)
+        put(2, 0)
+        add_z(3, 0)
+        put(2, 1)
+        add_z(2, 2)
+        put(3, 0)
+        seen0 = look(0, 0, PW, "slab1")
+        add_z(3, 1)
+        put(2, 2)
+        put(3, 1)
+        seen1 = look(1, 0, PW, "slab0")
+        weigh_all(0, seen0)
+        add_z(2, 3, "slab1", 1)
+        add_z(3, 2, "view0", 1)
+        put(2, 3)
+        put(3, 2)
+        seen2 = look(2, 0, PW, "seen2")
+        weigh_all(1, seen1)
+        add_z(3, 3, "slab0", 1)
+        w3_c = [shared([P, 512], U32, "slab%d" % (1 - g), 1) for g in range(2)]
+        w3_s = [held([P, 512], U8, "w3_s%d" % g) for g in range(2)]
+
+        def quantise_w3(g):
+            nc.vector.quantize_mx(out=w3_c[g][:].bitcast(E4M3), scales=w3_s[g][:], in_=w3_b[g][:])
+
+        quantise_w3(0)
+        put(3, 3)
+
+        seen_last = [look(3, 512 * half, 512, "seen3_%d" % half) for half in range(2)]
+        d_c = [held([P, PIECE], U32, "d_c%d" % n) for n in range(4)]
+        d_s = [held([P, PIECE], U8, "d_s%d" % n) for n in range(4)]
+        y_s = [held([P, 512], U8, "y_s%d" % half) for half in range(2)]
+        out_rows = out_0.rearrange("(g p t) j -> g p t j", g=2, t=4)
+
+        def weigh_last(n):
+            weigh(3, seen_last[n // 2], 512 * (n // 2), PIECE * n, PIECE)
+
+        def group_d(n):
+            d_b = shared([P, 4 * PIECE], BF16, "d_b", 2)
+            lo = PIECE * (n % 2)
+            interleave(nc.vector.tensor_copy, d_b[:], d_rows[n // 2][:, :, lo : lo + PIECE])
+            return d_b
+
+        def quantise_d(n, d_b):
+            nc.vector.quantize_mx(out=d_c[n][:].bitcast(E4M3), scales=d_s[n][:], in_=d_b[:])
+
+        def third_product(g, n, y, lo):
+            for pair in range(2):
+                yb = bank(("z", "mix")[pair])
+                for u in range(2):
+                    t = 2 * pair + u
+                    nc.tensor.matmul_mx(
+                        out=yb[:, PIECE * u : PIECE * (u + 1)],
+                        lhsT=w3_c[g][:, P * t : P * (t + 1)].bitcast(E4M3),
+                        lhsT_scale=w3_s[g][:, P * t : P * (t + 1)],
+                        rhs=d_c[n][:].bitcast(E4M3),
+                        rhs_scale=d_s[n][:],
+                        start=True,
+                        stop=True,
+                    )
+                nc.scalar.copy(
+                    out=y[:, 2 * pair : 2 * pair + 2, lo : lo + PIECE], in_=yb[:].rearrange("p (u j) -> p u j", u=2)
+                )
+
+        y_c = {}
+        for g in range(2):
+            for half in range(2):
+                y_c[g, half] = held([P, 512], U32, "y_c%d%d" % (g, half))
+
+        def group_y(y, lo):
+            y_b = shared([P, 4 * PIECE], BF16, "y_b", 2)
+            interleave(nc.vector.tensor_copy, y_b[:], y[:, :, lo : lo + PIECE])
+            return y_b
+
+        def quantise_y(g, n, y_b):
+            half, lo = n // 2, PIECE * (n % 2)
+            nc.vector.quantize_mx(
+                out=y_c[g, half][:, lo : lo + PIECE].bitcast(E4M3),
+                scales=y_s[half][4 * g : P, lo : lo + PIECE],
+                in_=y_b[:],
+            )
+
+        def store_words(g, half):
+            nc.sync.dma_start(
+                out=out_1[g].rearrange("p j i -> p (j i)").bitcast(I32)[:, 512 * half : 512 * (half + 1)],
+                in_=y_c[g, half][:].bitcast(I32),
+            )
+
+        def store_scales(half):
+            for q in range(4):
+                nc.sync.dma_start(
+                    out=out_2[:, 4 * q : 4 * q + 4, 512 * half : 512 * (half + 1)].bitcast(I32),
+                    in_=y_s[half][32 * q : 32 * q + 8, :].bitcast(I32),
+                )
+
+        weigh(2, seen2, 0, 0, 512)
+        weigh_last(0)
+        weigh_last(1)
+        d_b0 = group_d(0)
+        d_b1 = group_d(1)
+        quantise_d(0, d_b0)
+        quantise_w3(1)
+        quantise_d(1, d_b1)
+        weigh(2, seen2, 0, 512, 512)
+        weigh_last(2)
+        weigh_last(3)
+        d_b2 = group_d(2)
+        d_b3 = group_d(3)
+        quantise_d(2, d_b2)
+        quantise_d(3, d_b3)
+
+        pending = []
+        for n in range(2):
+            for g in range(2):
+                y = shared([P, 4, PIECE], F32, "quad", 4)
+                third_product(g, n, y, 0)
+                nc.sync.dma_start(out=out_rows[g][:, :, PIECE * n : PIECE * (n + 1)], in_=y[:])
+                pending.append((g, n, y, 0))
+        for g in range(2):
+            y = shared([P, 4, 512], F32, "wide%d" % g, 1)
+            for n in range(2, 4):
+                third_product(g, n, y, PIECE * (n - 2))
+                pending.append((g, n, y, PIECE * (n - 2)))
+            for pair in range(2):
+                nc.sync.dma_start(out=out_rows[g][:, 2 * pair : 2 * pair + 2, 512:1024], in_=y[:, 2 * pair : 2 * pair + 2, :])
+
+        grouped = group_y(pending[0][2], pending[0][3])
+        for k, (g, n, y, lo) in enumerate(pending):
+            current = grouped
+            if k + 1 < len(pending):
+                grouped = group_y(pending[k + 1][2], pending[k + 1][3])
+            quantise_y(g, n, current)
+            if n % 2 == 1:
+                store_words(g, n // 2)
+                if g == 1:
+                    store_scales(n // 2)

@@ -38,7 +38,7 @@ def tile_list_wiki_revision_patrol_kernel(
         def held(shape, dtype, name):
             return keep.tile(shape, dtype, name=name, align_bytes=64)
 
-        def shared(shape, dtype, tag, bufs):
+        def shared(shape, dtype, tag, bufs=1):
             return ring.tile(shape, dtype, name=tag, tag=tag, bufs=bufs, align_bytes=64)
 
         def bank(tag):
@@ -52,15 +52,10 @@ def tile_list_wiki_revision_patrol_kernel(
         w2_raw = held([P, 2 * H], U8, "w2_raw")
         nc.sync.dma_start(out=w2_raw[:].bitcast(I32), in_=w2_words[0].bitcast(I32))
         tab_w = [held([P, T], U32, "tab_w%d" % a) for a in range(2)]
-        w1_raw = [shared([P, 4, H], F32, "slab%d" % a, 1) for a in range(2)]
+        w1_raw = [shared([P, 4, H], F32, "slab%d" % a) for a in range(2)]
 
         def load_words(a):
             nc.sync.dma_start(out=tab_w[a][:].bitcast(I32), in_=tab_words[a].rearrange("p n i -> p (n i)").bitcast(I32))
-
-        load_words(0)
-        for a in range(2):
-            nc.sync.dma_start(out=w1_raw[a][:], in_=w1[512 * a : 512 * (a + 1), :].rearrange("(p i) r -> p i r", i=4))
-        load_words(1)
 
         tab_s = held([P, T], U8, "tab_s")
         w2_sraw = held([P, H], U8, "w2_sraw")
@@ -69,44 +64,41 @@ def tile_list_wiki_revision_patrol_kernel(
         base_t = held([P, 4], F32, "base_t")
         nc.gpsimd.memset(tab_s[:].bitcast(I32), 0)
         nc.gpsimd.memset(w2_sraw[:].bitcast(I32), 0)
+        load_words(0)
         for q in range(4):
-            nc.gpsimd.dma_start(
+            nc.sync.dma_start(
                 out=tab_s[32 * q : 32 * q + 8, :].bitcast(I32), in_=tab_scales[:, 4 * q : 4 * q + 4, :].bitcast(I32)
             )
+        for a in range(2):
+            nc.sync.dma_start(out=w1_raw[a][:], in_=w1[512 * a : 512 * (a + 1), :].rearrange("(p i) r -> p i r", i=4))
         for q in range(4):
-            nc.gpsimd.dma_start(
+            nc.sync.dma_start(
                 out=w2_sraw[32 * q : 32 * q + 4, :].bitcast(I32), in_=w2_scales[0, 4 * q : 4 * q + 4, :].bitcast(I32)
             )
-        nc.gpsimd.dma_start(out=gain_t[:], in_=gain.rearrange("(p t) -> p t", t=4))
-        nc.gpsimd.dma_start(out=vthr_t[:], in_=vthr.rearrange("(p t) -> p t", t=4))
-        nc.gpsimd.dma_start(out=base_t[:], in_=base.rearrange("(p t) -> p t", t=4))
-
+        load_words(1)
+        nc.sync.dma_start(out=gain_t[:], in_=gain.rearrange("(p t) -> p t", t=4))
+        nc.sync.dma_start(out=base_t[:], in_=base.rearrange("(p t) -> p t", t=4))
         nc.sync.dma_start(idx2[:], offs2)
+        minus_base = held([P, 4], F32, "minus_base")
+        nc.gpsimd.tensor_scalar(out=minus_base[:], in0=base_t[:], scalar1=-1.0, scalar2=0.0, op0=ALU.mult, op1=ALU.add)
+
         wgs_rows = wgs.rearrange("(q t) j -> q t j", t=4)
         page_rows = page0.rearrange("(p t) c -> p t c", t=4)
-        view_rows = view.rearrange("(p t) j -> p t j", t=4)
 
-        def load_wgs(tile, t0, count, start):
+        def load_wgs(tag, start, count):
+            tile = shared([P, 4, count], F32, tag)
             for q in (0, 2, 1, 3):
-                nc.sync.dma_start(
-                    out=tile[32 * q : 32 * q + 32, :, :], in_=wgs_rows[:, t0 : t0 + count, start : start + 512]
-                )
+                nc.sync.dma_start(out=tile[32 * q : 32 * q + 32, :, :], in_=wgs_rows[:, :, start : start + count])
+            return tile
 
-        page = [held([P, T2], F32, "page%d" % t) for t in range(4)]
-        wg_first = [shared([P, 2, 512], F32, "quad", 4) for pair in range(2)]
-        wg_second = shared([P, 4, 512], F32, "wide0", 1)
-        for pair in range(2):
-            load_wgs(wg_first[pair], 2 * pair, 2, 0)
-            for t in (2 * pair, 2 * pair + 1):
-                nc.sync.dma_start(out=page[t][:], in_=page_rows[:, t, :])
-        load_wgs(wg_second, 0, 4, 512)
+        page = [shared([P, T2], F32, "page%d" % t) for t in range(4)]
+        wg0 = load_wgs("wg0", 0, PIECE)
+        for t in range(4):
+            nc.sync.dma_start(out=page[t][:], in_=page_rows[:, t, :])
+        wg1 = load_wgs("wg1", PIECE, PIECE)
+        wg2 = load_wgs("wg2", 2 * PIECE, 2 * PIECE)
         nc.sync.dma_start(idx3[:], offs3)
-
-        def wgs_for(c, t):
-            lo = PIECE * (c % 2)
-            if c < 2:
-                return wg_first[t // 2][:, t % 2, lo : lo + PIECE]
-            return wg_second[:, t, lo : lo + PIECE]
+        nc.sync.dma_start(out=vthr_t[:], in_=vthr.rearrange("(p t) -> p t", t=4))
 
         w2_c = held([P, 2 * H], U8, "w2_c")
         w2_s = held([P, H], U8, "w2_s")
@@ -128,24 +120,22 @@ def tile_list_wiki_revision_patrol_kernel(
 
         w1_c = [held([P, H], U32, "w1_c%d" % a) for a in range(2)]
         w1_s = [held([P, H], U8, "w1_s%d" % a) for a in range(2)]
-        w1_b = [shared([P, 4 * H], BF16, "wb", 2) for a in range(2)]
+        w1_b = [shared([P, 4 * H], BF16, "wb%d" % a) for a in range(2)]
         deal_columns(nc.scalar.copy, w1_b[0], w1_raw[0], 0, 128)
         nc.vector.quantize_mx(out=w1_c[0][:].bitcast(E4M3), scales=w1_s[0][:], in_=w1_b[0][:])
         deal_columns(nc.scalar.copy, w1_b[1], w1_raw[1], 0, 64)
         deal_columns(nc.vector.tensor_copy, w1_b[1], w1_raw[1], 64, 128)
         nc.vector.quantize_mx(out=w1_c[1][:].bitcast(E4M3), scales=w1_s[1][:], in_=w1_b[1][:])
 
+        def gather_words(out, start, count):
+            nc.vector.tensor_copy(out, tab_w[1][:].indirect(entries(idx1, start, count)))
+
         got_w1 = {}
 
-        def gather_words(first, count, tile):
-            nc.vector.tensor_copy(tile[:], tab_w[1][:].indirect(entries(idx1, PIECE * first, PIECE * count)))
-            for k in range(count):
-                got_w1[first + k] = tile[:, PIECE * k : PIECE * (k + 1)]
-
-        def first_product(out, t, a, c, lo, width, start, stop):
-            j0 = PIECE * c + lo
-            moving = got_w0[:, j0 : j0 + width] if a == 0 else got_w1[c][:, lo : lo + width]
-            if c == 0:
+        def first_product(out, t, a, chunk, lo, width, start, stop):
+            j0 = chunk + lo
+            moving = got_w0[:, j0 : j0 + width] if a == 0 else got_w1[chunk][:, lo : lo + width]
+            if chunk == 0:
                 scales = got_s_first[4 * a : P, j0 : j0 + width]
             else:
                 scales = got_s_rest[4 * a : P, j0 - PIECE : j0 - PIECE + width]
@@ -170,14 +160,37 @@ def tile_list_wiki_revision_patrol_kernel(
                 stop=stop,
             )
 
-        def interleave(engine_copy, grouped, rows):
-            engine_copy(
-                out=grouped.rearrange("p (c i t) -> p c t i", i=4, t=4),
-                in_=rows.rearrange("p t (c i) -> p c t i", i=4),
-            )
+        def by_runs(rows):
+            return rows.rearrange("p t (c i) -> p c t i", i=4)
 
-        gather_words(0, 1, held([P, PIECE], U32, "got_w1_0"))
-        gather_words(1, 1, held([P, PIECE], U32, "got_w1_1"))
+        def side_by_side(grouped):
+            return grouped.rearrange("p (c i t) -> p c t i", i=4, t=4)
+
+        def interleave(engine_copy, grouped, rows):
+            engine_copy(out=side_by_side(grouped), in_=by_runs(rows))
+
+        def quantise(codes, scales, grouped):
+            nc.vector.quantize_mx(out=codes.bitcast(E4M3), scales=scales, in_=grouped)
+
+        def bend(zb):
+            th = shared([P, BANK], F32, "th", 4)
+            nc.scalar.activation(out=th[:], in_=zb[:], func=ACT.Tanh)
+            return th
+
+        def apply_gain(out, th, t):
+            nc.scalar.activation(out=out, in_=th, func=ACT.Copy, scale=gain_t[:, t : t + 1])
+
+        def add_z(out, pb, z):
+            nc.vector.tensor_tensor(out=out, in0=pb, in1=z, op=ALU.add)
+
+        def put(t, start, h, weights):
+            nc.vector.tensor_tensor(page[t][:].indirect(entries(idx2, start, h.shape[1])), h, weights, ALU.mult)
+
+        got_w1[0] = held([P, PIECE], U32, "got_w1_0")
+        got_w1[PIECE] = held([P, PIECE], U32, "got_w1_1")
+        for half in range(2):
+            gather_words(got_w1[0][:, P * half : P * (half + 1)], P * half, P)
+        gather_words(got_w1[PIECE][:], PIECE, PIECE)
         nc.vector.tensor_copy(
             out=w2_s[:].rearrange("p (t q) -> p q t", t=4), in_=w2_sraw[:].rearrange("p (q t) -> p q t", t=4)
         )
@@ -191,21 +204,14 @@ def tile_list_wiki_revision_patrol_kernel(
                     )
         bent = []
         for half in range(2):
-            th = shared([P, BANK], F32, "th", 3)
+            th = shared([P, BANK], F32, "th", 4)
             nc.scalar.activation(
                 out=th[:].rearrange("p (j t) -> p j t", t=4),
                 in_=z_banks[half][:].rearrange("p (t j) -> p j t", t=4),
                 func=ACT.Tanh,
             )
             bent.append(th)
-        z_sb = {}
-        z_sb[0, 1] = held([P, 2, PIECE], F32, "z_01")
-        for half in range(2):
-            nc.scalar.copy(
-                out=z_sb[0, 1][:, :, P * half : P * (half + 1)],
-                in_=z_banks[half][:, 2 * P : 4 * P].rearrange("p (t j) -> p t j", t=2),
-            )
-        f_half = [held([P, 4 * P], BF16, "f_half%d" % half) for half in range(2)]
+        f_half = [shared([P, 4 * P], BF16, "f_half%d" % half) for half in range(2)]
         f_c0 = [held([P, P], U32, "f_c0_%d" % half) for half in range(2)]
         f_s0 = [held([P, P], U8, "f_s0_%d" % half) for half in range(2)]
         for half in range(2):
@@ -216,272 +222,250 @@ def tile_list_wiki_revision_patrol_kernel(
                 op=ALU.mult,
             )
         for half in range(2):
-            nc.vector.quantize_mx(out=f_c0[half][:].bitcast(E4M3), scales=f_s0[half][:], in_=f_half[half][:])
-
-        mixed = {}
-        h_pair = {}
-
-        def mix(c, operands):
-            for pair in range(2):
-                pb = bank("mix")
-                summed = c < 2 and pair == 0
-                if summed:
-                    for u in range(2):
-                        for a in range(2):
-                            first_product(
-                                pb[:, PIECE * u : PIECE * (u + 1)], u, a, c, 0, PIECE, start=(u == 0 and a == 0), stop=False
-                            )
-                for k, (codes, scales, lo, width) in enumerate(operands):
-                    for u in range(2):
-                        col = PIECE * u + lo
-                        last = k == len(operands) - 1 and u == 1
-                        second_product(
-                            pb[:, col : col + width], 2 * pair + u, codes, scales,
-                            start=not summed, stop=last or not summed,
-                        )
-                if summed:
-                    h_pair[c] = shared([P, BANK], F32, ("after1", "h_pair1")[c], 1)
-                    nc.scalar.copy(out=h_pair[c][:], in_=pb[:])
-                else:
-                    mixed[c, pair] = pb
-
-        mix(0, [(f_c0[half][:], f_s0[half][:], P * half, P) for half in range(2)])
-
-        def prepare(c):
-            f_rows = shared([P, 4, PIECE], BF16, "f_rows", 2)
-            for pair in range(2):
-                zb = bank("z")
+            quantise(f_c0[half][:], f_s0[half][:], f_half[half][:])
+        h_banks = [bank("mix"), bank("mix")]
+        for pair in range(2):
+            for a in range(2):
                 for u in range(2):
-                    for a in range(2):
-                        first_product(
-                            zb[:, PIECE * u : PIECE * (u + 1)], 2 * pair + u, a, c, 0, PIECE, start=(a == 0), stop=(a == 1)
-                        )
-                th = shared([P, BANK], F32, "th", 3)
-                nc.scalar.activation(out=th[:], in_=zb[:], func=ACT.Tanh)
-                if c >= 2 or pair == 1:
-                    z_sb[c, pair] = held([P, 2, PIECE], F32, "z_%d%d" % (c, pair))
-                    nc.scalar.copy(out=z_sb[c, pair][:].rearrange("p t j -> p (t j)"), in_=zb[:])
-                for u in range(2):
-                    t = 2 * pair + u
-                    nc.scalar.activation(
-                        out=f_rows[:, t, :], in_=th[:, PIECE * u : PIECE * (u + 1)], func=ACT.Copy, scale=gain_t[:, t : t + 1]
+                    first_product(
+                        h_banks[pair][:, PIECE * u : PIECE * (u + 1)], 2 * pair + u, a, 0, 0, PIECE,
+                        start=(u == 0 and a == 0), stop=False,
                     )
-            f_b = shared([P, 4 * PIECE], BF16, "hold%d" % c, 1)
-            interleave(nc.scalar.copy, f_b[:], f_rows[:])
-            return f_b
+        for half in range(2):
+            for pair in range(2):
+                for u in range(2):
+                    col = PIECE * u + P * half
+                    second_product(
+                        h_banks[pair][:, col : col + P], 2 * pair + u, f_c0[half][:], f_s0[half][:],
+                        start=False, stop=(half == 1 and u == 1),
+                    )
 
-        def quantise_f(c, f_b):
-            f_c = shared([P, PIECE], U32, "after%d" % c, 1)
-            f_s = held([P, PIECE], U8, "f_s%d" % c)
-            nc.vector.quantize_mx(out=f_c[:].bitcast(E4M3), scales=f_s[:], in_=f_b[:])
-            mix(c, [(f_c[:], f_s[:], 0, PIECE)])
+        def empty_h(t, tag):
+            h = shared([P, PIECE], F32, tag)
+            nc.scalar.copy(out=h[:], in_=h_banks[t // 2][:, PIECE * (t % 2) : PIECE * (t % 2 + 1)])
+            return h
 
-        h_rows = {}
+        h0 = [empty_h(t, "h0%d" % t) for t in range(3)]
+        got_w1[2 * PIECE] = shared([P, 2 * PIECE], U32, "f_half1")
+        gather_words(got_w1[2 * PIECE][:], 2 * PIECE, 2 * PIECE)
 
-        def add_z(c, t, tag="h", bufs=3):
-            h = shared([P, PIECE], F32, tag, bufs)
-            u = t % 2
-            nc.vector.tensor_tensor(
-                out=h[:], in0=mixed[c, t // 2][:, PIECE * u : PIECE * (u + 1)], in1=z_sb[c, t // 2][:, u, :], op=ALU.add
-            )
-            h_rows[c, t] = h[:]
+        f_rows1 = shared([P, 4, PIECE], BF16, "f_rows1")
+        z1_banks = []
+        for pair in range(2):
+            zb = bank("z")
+            for u in range(2):
+                for a in range(2):
+                    first_product(
+                        zb[:, PIECE * u : PIECE * (u + 1)], 2 * pair + u, a, PIECE, 0, PIECE, start=(a == 0), stop=(a == 1)
+                    )
+            th = bend(zb)
+            for u in range(2):
+                apply_gain(f_rows1[:, 2 * pair + u, :], th[:, PIECE * u : PIECE * (u + 1)], 2 * pair + u)
+            z1_banks.append(zb)
+        f_b1 = held([P, 4 * PIECE], BF16, "f_b1")
+        interleave(nc.scalar.copy, f_b1[:], f_rows1[:])
+        h0.append(empty_h(3, "f_rows1"))
+        z1 = [held([P, BANK], F32, "z1_%d" % pair) for pair in range(2)]
+        for pair in range(2):
+            nc.scalar.copy(out=z1[pair][:], in_=z1_banks[pair][:])
 
-        def put(c, t):
-            if c < 2 and t < 2:
-                h = h_pair[c][:, PIECE * t : PIECE * (t + 1)]
-            else:
-                h = h_rows[c, t]
-            nc.vector.tensor_tensor(page[t][:].indirect(entries(idx2, PIECE * c, PIECE)), h, wgs_for(c, t), ALU.mult)
+        f_rows2 = shared([P, 4, BANK], BF16, "wb0")
+        z2_banks = []
+        for t in range(4):
+            zb = bank("z")
+            for a in range(2):
+                first_product(zb[:], t, a, 2 * PIECE, 0, BANK, start=(a == 0), stop=(a == 1))
+            apply_gain(f_rows2[:, t, :], bend(zb)[:], t)
+            z2_banks.append(zb)
+        f_b2 = shared([P, 4 * BANK], BF16, "wb1")
+        interleave(nc.scalar.copy, f_b2[:], f_rows2[:])
+        z2 = [held([P, BANK], F32, "z2_%d" % t) for t in range(4)]
+        for t in range(4):
+            nc.scalar.copy(out=z2[t][:], in_=z2_banks[t][:])
+
+        w3_raw = [shared([P, 4, BANK], F32, "slab%d" % g) for g in range(2)]
+        for g in range(2):
+            nc.sync.dma_start(out=w3_raw[g][:], in_=w3.rearrange("(p i) n -> p i n", i=4)[:, :, 512 * g : 512 * (g + 1)])
+        view_t = held([P, 4, PW], F32, "view_t")
+        nc.sync.dma_start(out=view_t[:], in_=view.rearrange("(p t) j -> p t j", t=4))
+        w3_b = [shared([P, 4 * BANK], BF16, "wb0")]
+        deal_columns(nc.scalar.copy, w3_b[0], w3_raw[0], 0, 128)
+
+        for t in range(3):
+            put(t, 0, h0[t][:], wg0[:, t, :])
+        f_c1 = shared([P, PIECE], U32, "h01")
+        f_s1 = held([P, PIECE], U8, "f_s1")
+        quantise(f_c1[:], f_s1[:], f_b1[:])
+        mix1 = [bank("mix"), bank("mix")]
+        for t in range(4):
+            col = PIECE * (t % 2)
+            second_product(mix1[t // 2][:, col : col + PIECE], t, f_c1[:], f_s1[:], start=True, stop=True)
+        put(3, 0, h0[3][:], wg0[:, 3, :])
+        h1_pair = shared([P, BANK], F32, "h1_pair")
+        h12 = held([P, PIECE], F32, "h12")
+        add_z(h1_pair[:], mix1[0][:], z1[0][:])
+        add_z(h12[:], mix1[1][:, 0:PIECE], z1[1][:, 0:PIECE])
+        for t in range(2):
+            put(t, PIECE, h1_pair[:, PIECE * t : PIECE * (t + 1)], wg1[:, t, :])
+        put(2, PIECE, h12[:], wg1[:, 2, :])
+        f_c2 = shared([P, BANK], U32, "h1_pair")
+        f_s2 = held([P, BANK], U8, "f_s2")
+        quantise(f_c2[:], f_s2[:], f_b2[:])
+        h13 = shared([P, PIECE], F32, "wb1")
+        add_z(h13[:], mix1[1][:, PIECE:BANK], z1[1][:, PIECE:BANK])
+        put(3, PIECE, h13[:], wg1[:, 3, :])
+        w3_b.append(shared([P, 4 * BANK], BF16, "wb1"))
+        deal_columns(nc.scalar.copy, w3_b[1], w3_raw[1], 0, 128)
+
+        mix2 = []
+        for t in range(4):
+            pb = bank("mix")
+            second_product(pb[:], t, f_c2[:], f_s2[:], start=True, stop=True)
+            mix2.append(pb)
+
+        centred = held([P, 4, PW], F32, "centred")
 
         def look(t, start, count, tag):
-            seen = shared([P, count], F32, tag, 1)
+            seen = shared([P, count], F32, tag)
             nc.scalar.activation(
                 out=seen[:], in_=page[t][:].indirect(entries(idx3, start, count)), func=ACT.Sigmoid, bias=vthr_t[:, t : t + 1]
             )
             return seen
 
-        d_rows = [held([P, 4, 512], BF16, "d_rows%d" % half) for half in range(2)]
-        view_t = [shared([P, PW], F32, "view%d" % t, 1) for t in range(4)]
-
-        def weigh(t, seen, seen_start, start, count):
-            half, lo = divmod(start, 512)
-            nc.vector.scalar_tensor_tensor(
-                out=d_rows[half][:, t, lo : lo + count],
-                in0=seen[:, start - seen_start : start - seen_start + count],
-                scalar=base_t[:, t : t + 1],
-                in1=view_t[t][:, start : start + count],
-                op0=ALU.subtract,
-                op1=ALU.mult,
+        def centre(t, start, seen):
+            nc.scalar.activation(
+                out=centred[:, t, start : start + seen.shape[1]], in_=seen, func=ACT.Identity, bias=minus_base[:, t : t + 1]
             )
 
-        def weigh_all(t, seen):
-            for half in range(2):
-                weigh(t, seen, 0, 512 * half, 512)
+        h2 = {}
 
-        f_b1 = prepare(1)
-        put(0, 0)
-        put(0, 1)
-        quantise_f(1, f_b1)
-        gather_words(2, 2, shared([P, 2 * PIECE], U32, "hold1", 1))
-        f_b2 = prepare(2)
-        f_b3 = prepare(3)
+        def add_last(t):
+            h2[t] = shared([P, BANK], F32, "h2_%d" % (t % 2))
+            add_z(h2[t][:], mix2[t][:], z2[t][:])
 
-        w3_b = []
+        def put_last(t):
+            put(t, 2 * PIECE, h2[t][:], wg2[:, t, :])
+
+        add_last(0)
+        add_last(1)
+        put_last(0)
+        centre(0, 0, look(0, 0, PW, "slab1")[:])
+        add_last(2)
+        put_last(1)
+        centre(1, 0, look(1, 0, PW, "page0")[:])
+        add_last(3)
+        put_last(2)
+        seen2 = look(2, 0, PW, "page1")
+        centre(2, 0, seen2[:, 0:BANK])
+        put_last(3)
+        w3_c = [shared([P, BANK], U32, ("h2_1", "wg2")[g]) for g in range(2)]
+        w3_s = [held([P, BANK], U8, "w3_s%d" % g) for g in range(2)]
         for g in range(2):
-            raw = shared([P, 4, 512], F32, "slab%d" % g, 1)
-            nc.sync.dma_start(out=raw[:], in_=w3.rearrange("(p i) n -> p i n", i=4)[:, :, 512 * g : 512 * (g + 1)])
-            grouped = shared([P, 4 * 512], BF16, "wb", 2)
-            deal_columns(nc.scalar.copy, grouped, raw, 0, 128)
-            w3_b.append(grouped)
-        for t in range(4):
-            nc.sync.dma_start(out=view_t[t][:], in_=view_rows[:, t, :])
+            quantise(w3_c[g][:], w3_s[g][:], w3_b[g][:])
+        nc.vector.tensor_scalar(
+            out=centred[:, 2, BANK:PW], in0=seen2[:, BANK:PW], scalar1=base_t[:, 2:3], scalar2=None, op0=ALU.subtract
+        )
+        for half in range(2):
+            centre(3, BANK * half, look(3, BANK * half, BANK, "page2")[:])
 
-        put(1, 0)
-        add_z(0, 2, "after2", 1)
-        put(1, 1)
-        add_z(0, 3)
-        put(0, 2)
-        quantise_f(2, f_b2)
-        add_z(1, 2, "hold2", 1)
-        put(0, 3)
-        add_z(1, 3, "after3", 1)
-        put(1, 2)
-        add_z(2, 0)
-        put(1, 3)
-        quantise_f(3, f_b3)
-        add_z(2, 1, "hold3", 1)
-        put(2, 0)
-        add_z(3, 0)
-        put(2, 1)
-        add_z(2, 2)
-        put(3, 0)
-        seen0 = look(0, 0, PW, "slab1")
-        add_z(3, 1)
-        put(2, 2)
-        put(3, 1)
-        seen1 = look(1, 0, PW, "slab0")
-        weigh_all(0, seen0)
-        add_z(2, 3, "slab1", 1)
-        add_z(3, 2, "view0", 1)
-        put(2, 3)
-        put(3, 2)
-        seen2 = look(2, 0, PW, "seen2")
-        weigh_all(1, seen1)
-        add_z(3, 3, "slab0", 1)
-        w3_c = [shared([P, 512], U32, "slab%d" % (1 - g), 1) for g in range(2)]
-        w3_s = [held([P, 512], U8, "w3_s%d" % g) for g in range(2)]
+        starts = (0, P, PIECE, BANK)
+        widths = (P, P, PIECE, BANK)
+        d_b = [held([P, 4 * w], BF16, "d_b%d" % n) for n, w in enumerate(widths)]
+        d_c = [held([P, w], U32, "d_c%d" % n) for n, w in enumerate(widths)]
+        d_s = [held([P, w], U8, "d_s%d" % n) for n, w in enumerate(widths)]
 
-        def quantise_w3(g):
-            nc.vector.quantize_mx(out=w3_c[g][:].bitcast(E4M3), scales=w3_s[g][:], in_=w3_b[g][:])
+        def weigh(n, lo, count):
+            cols = slice(starts[n] + lo, starts[n] + lo + count)
+            nc.vector.tensor_tensor(
+                out=side_by_side(d_b[n][:, 4 * lo : 4 * (lo + count)]),
+                in0=by_runs(centred[:, :, cols]),
+                in1=by_runs(view_t[:, :, cols]),
+                op=ALU.mult,
+            )
 
-        quantise_w3(0)
-        put(3, 3)
+        def quantise_d(n):
+            quantise(d_c[n][:], d_s[n][:], d_b[n][:])
 
-        seen_last = [look(3, 512 * half, 512, "seen3_%d" % half) for half in range(2)]
-        d_c = [held([P, PIECE], U32, "d_c%d" % n) for n in range(4)]
-        d_s = [held([P, PIECE], U8, "d_s%d" % n) for n in range(4)]
-        y_s = [held([P, 512], U8, "y_s%d" % half) for half in range(2)]
+        weigh(0, 0, P)
+        weigh(1, 0, P)
+        quantise_d(0)
+        quantise_d(1)
+        weigh(2, 0, PIECE)
+        weigh(3, 0, PIECE)
+        quantise_d(2)
+        weigh(3, PIECE, PIECE)
+        quantise_d(3)
+
+        y = {}
+        for half in range(2):
+            for g in range(2):
+                y[g, half] = shared([P, 4, BANK], F32, (("slab0", "slab1"), ("page2", "page3"))[half][g])
+        y_c = {key: held([P, BANK], U32, "y_c%d%d" % key) for key in y}
+        y_s = [held([P, BANK], U8, "y_s%d" % half) for half in range(2)]
         out_rows = out_0.rearrange("(g p t) j -> g p t j", g=2, t=4)
 
-        def weigh_last(n):
-            weigh(3, seen_last[n // 2], 512 * (n // 2), PIECE * n, PIECE)
-
-        def group_d(n):
-            d_b = shared([P, 4 * PIECE], BF16, "d_b", 2)
-            lo = PIECE * (n % 2)
-            interleave(nc.vector.tensor_copy, d_b[:], d_rows[n // 2][:, :, lo : lo + PIECE])
-            return d_b
-
-        def quantise_d(n, d_b):
-            nc.vector.quantize_mx(out=d_c[n][:].bitcast(E4M3), scales=d_s[n][:], in_=d_b[:])
-
-        def third_product(g, n, y, lo):
-            for pair in range(2):
-                yb = bank(("z", "mix")[pair])
-                for u in range(2):
-                    t = 2 * pair + u
-                    nc.tensor.matmul_mx(
-                        out=yb[:, PIECE * u : PIECE * (u + 1)],
-                        lhsT=w3_c[g][:, P * t : P * (t + 1)].bitcast(E4M3),
-                        lhsT_scale=w3_s[g][:, P * t : P * (t + 1)],
-                        rhs=d_c[n][:].bitcast(E4M3),
-                        rhs_scale=d_s[n][:],
-                        start=True,
-                        stop=True,
-                    )
-                nc.scalar.copy(
-                    out=y[:, 2 * pair : 2 * pair + 2, lo : lo + PIECE], in_=yb[:].rearrange("p (u j) -> p u j", u=2)
+        def third_product(g, n, first, count, tag):
+            width = widths[n]
+            half, lo = divmod(starts[n], BANK)
+            yb = bank(tag)
+            for u in range(count):
+                t = first + u
+                nc.tensor.matmul_mx(
+                    out=yb[:, width * u : width * (u + 1)],
+                    lhsT=w3_c[g][:, P * t : P * (t + 1)].bitcast(E4M3),
+                    lhsT_scale=w3_s[g][:, P * t : P * (t + 1)],
+                    rhs=d_c[n][:].bitcast(E4M3),
+                    rhs_scale=d_s[n][:],
+                    start=True,
+                    stop=True,
                 )
+            nc.scalar.copy(
+                out=y[g, half][:, first : first + count, lo : lo + width], in_=yb[:].rearrange("p (u j) -> p u j", u=count)
+            )
 
-        y_c = {}
+        def store_y(g, half, rows, lo, count):
+            nc.sync.dma_start(
+                out=out_rows[g][:, rows, BANK * half + lo : BANK * half + lo + count], in_=y[g, half][:, rows, lo : lo + count]
+            )
+
         for g in range(2):
-            for half in range(2):
-                y_c[g, half] = held([P, 512], U32, "y_c%d%d" % (g, half))
+            for n in range(2):
+                third_product(g, n, 0, 4, ("z", "mix")[n])
+            store_y(g, 0, slice(0, 4), 0, PIECE)
+        for g in range(2):
+            for pair in range(2):
+                third_product(g, 2, 2 * pair, 2, ("z", "mix")[pair])
+            store_y(g, 0, slice(0, 4), PIECE, PIECE)
+        for g in range(2):
+            for t in range(4):
+                third_product(g, 3, t, 1, ("z", "mix")[t % 2])
+                if t % 2 == 1:
+                    store_y(g, 1, slice(t - 1, t + 1), 0, BANK)
 
-        def group_y(y, lo):
-            y_b = shared([P, 4 * PIECE], BF16, "y_b", 2)
-            interleave(nc.vector.tensor_copy, y_b[:], y[:, :, lo : lo + PIECE])
+        order = [(g, 0, lo) for lo in (0, PIECE) for g in range(2)] + [(g, 1, lo) for g in range(2) for lo in (0, PIECE)]
+
+        def group_y(k):
+            g, half, lo = order[k]
+            y_b = shared([P, 4 * PIECE], BF16, "y_b", 3)
+            engine_copy = nc.scalar.copy if k == len(order) - 1 else nc.vector.tensor_copy
+            interleave(engine_copy, y_b[:], y[g, half][:, :, lo : lo + PIECE])
             return y_b
 
-        def quantise_y(g, n, y_b):
-            half, lo = n // 2, PIECE * (n % 2)
-            nc.vector.quantize_mx(
-                out=y_c[g, half][:, lo : lo + PIECE].bitcast(E4M3),
-                scales=y_s[half][4 * g : P, lo : lo + PIECE],
-                in_=y_b[:],
-            )
-
-        def store_words(g, half):
-            nc.sync.dma_start(
-                out=out_1[g].rearrange("p j i -> p (j i)").bitcast(I32)[:, 512 * half : 512 * (half + 1)],
-                in_=y_c[g, half][:].bitcast(I32),
-            )
-
-        def store_scales(half):
-            for q in range(4):
-                nc.sync.dma_start(
-                    out=out_2[:, 4 * q : 4 * q + 4, 512 * half : 512 * (half + 1)].bitcast(I32),
-                    in_=y_s[half][32 * q : 32 * q + 8, :].bitcast(I32),
-                )
-
-        weigh(2, seen2, 0, 0, 512)
-        weigh_last(0)
-        weigh_last(1)
-        d_b0 = group_d(0)
-        d_b1 = group_d(1)
-        quantise_d(0, d_b0)
-        quantise_w3(1)
-        quantise_d(1, d_b1)
-        weigh(2, seen2, 0, 512, 512)
-        weigh_last(2)
-        weigh_last(3)
-        d_b2 = group_d(2)
-        d_b3 = group_d(3)
-        quantise_d(2, d_b2)
-        quantise_d(3, d_b3)
-
-        pending = []
-        for n in range(2):
-            for g in range(2):
-                y = shared([P, 4, PIECE], F32, "quad", 4)
-                third_product(g, n, y, 0)
-                nc.sync.dma_start(out=out_rows[g][:, :, PIECE * n : PIECE * (n + 1)], in_=y[:])
-                pending.append((g, n, y, 0))
-        for g in range(2):
-            y = shared([P, 4, 512], F32, "wide%d" % g, 1)
-            for n in range(2, 4):
-                third_product(g, n, y, PIECE * (n - 2))
-                pending.append((g, n, y, PIECE * (n - 2)))
-            for pair in range(2):
-                nc.sync.dma_start(out=out_rows[g][:, 2 * pair : 2 * pair + 2, 512:1024], in_=y[:, 2 * pair : 2 * pair + 2, :])
-
-        grouped = group_y(pending[0][2], pending[0][3])
-        for k, (g, n, y, lo) in enumerate(pending):
+        grouped = group_y(0)
+        for k, (g, half, lo) in enumerate(order):
             current = grouped
-            if k + 1 < len(pending):
-                grouped = group_y(pending[k + 1][2], pending[k + 1][3])
-            quantise_y(g, n, current)
-            if n % 2 == 1:
-                store_words(g, n // 2)
+            if k + 1 < len(order):
+                grouped = group_y(k + 1)
+            quantise(y_c[g, half][:, lo : lo + PIECE], y_s[half][4 * g : P, lo : lo + PIECE], current[:])
+            if lo == PIECE:
+                nc.sync.dma_start(
+                    out=out_1[g].rearrange("p j i -> p (j i)").bitcast(I32)[:, BANK * half : BANK * (half + 1)],
+                    in_=y_c[g, half][:].bitcast(I32),
+                )
                 if g == 1:
-                    store_scales(n // 2)
+                    for q in range(4):
+                        queue = nc.scalar if half == 1 and q % 2 == 1 else nc.sync
+                        queue.dma_start(
+                            out=out_2[:, 4 * q : 4 * q + 4, BANK * half : BANK * (half + 1)].bitcast(I32),
+                            in_=y_s[half][32 * q : 32 * q + 8, :].bitcast(I32),
+                        )

@@ -48,6 +48,11 @@ def tile_list_wiki_revision_patrol_kernel(
         idx2 = keep.tile([P, S // 16], U16, name="idx2")
         idx3 = keep.tile([P, PW // 16], U16, name="idx3")
 
+        warm_in = held([P, 1], F32, "warm_in")
+        warm_out = held([P, 1], F32, "warm_out")
+        nc.vector.memset(warm_in[:], 0.0)
+        nc.scalar.activation(out=warm_out[:], in_=warm_in[:], func=ACT.Sigmoid)
+
         nc.sync.dma_start(idx1[:], offs)
         w2_raw = held([P, 2 * H], U8, "w2_raw")
         nc.sync.dma_start(out=w2_raw[:].bitcast(I32), in_=w2_words[0].bitcast(I32))

from contextlib import ExitStack

import concourse.mybir as mybir

K, T, S, H, T2, PW, N = 1024, 2048, 1024, 512, 2048, 1024, 1024
FLOPS = 2 * K * H * S + 2 * H * H * S + 2 * H * N * PW

F32 = mybir.dt.float32
BF16 = mybir.dt.bfloat16
I32 = mybir.dt.int32
U32 = mybir.dt.uint32
U16 = mybir.dt.uint16
U8 = mybir.dt.uint8
E4M3 = mybir.dt.float8_e4m3fn_x4
E2M1 = mybir.dt.float4_e2m1fn_x4
ACT = mybir.ActivationFunctionType
ALU = mybir.AluOpType

P = 128
BANK = 512
PIECE = 256


def entries(offsets, start, count):
    return offsets[:, start // 16 : (start + count) // 16]


def tile_list_wiki_revision_patrol_kernel(
    tc, tab_words, tab_scales, offs, offs2, offs3, w1, gain, w2_words, w2_scales, page0, wgs, vthr, base, view, w3,
    out_0, out_1, out_2,
):
    nc = tc.nc
    with ExitStack() as ctx:
        keep = ctx.enter_context(tc.tile_pool(name="keep", bufs=1))
        ring = ctx.enter_context(tc.tile_pool(name="ring", bufs=2))
        psum = ctx.enter_context(tc.psum_pool(name="psum", bufs=4))

        def held(shape, dtype, name):
            return keep.tile(shape, dtype, name=name, align_bytes=64)

        def shared(shape, dtype, tag, bufs=1):
            return ring.tile(shape, dtype, name=tag, tag=tag, bufs=bufs, align_bytes=64)

        def bank(tag):
            return psum.tile([P, BANK], F32, name=tag, tag=tag)

        idx1 = keep.tile([P, S // 16], U16, name="idx1")
        idx2 = keep.tile([P, S // 16], U16, name="idx2")
        idx3 = keep.tile([P, PW // 16], U16, name="idx3")

        warm_in = held([P, 1], F32, "warm_in")
        warm_out = held([P, 1], F32, "warm_out")
        nc.vector.memset(warm_in[:], 0.0)
        nc.scalar.activation(out=warm_out[:], in_=warm_in[:], func=ACT.Sigmoid)

        nc.sync.dma_start(idx1[:], offs)
        w2_raw = held([P, 2 * H], U8, "w2_raw")
        nc.sync.dma_start(out=w2_raw[:].bitcast(I32), in_=w2_words[0].bitcast(I32))
        tab_w = [held([P, T], U32, "tab_w%d" % a) for a in range(2)]
        w1_raw = [shared([P, 4, H], F32, "slab%d" % a) for a in range(2)]

        def load_words(a):
            nc.sync.dma_start(out=tab_w[a][:].bitcast(I32), in_=tab_words[a].rearrange("p n i -> p (n i)").bitcast(I32))

        tab_s = held([P, T], U8, "tab_s")
        w2_sraw = held([P, H], U8, "w2_sraw")
        gain_t = held([P, 4], F32, "gain_t")
        vthr_t = held([P, 4], F32, "vthr_t")
        base_t = held([P, 4], F32, "base_t")
        nc.gpsimd.memset(tab_s[:].bitcast(I32), 0)
        nc.gpsimd.memset(w2_sraw[:].bitcast(I32), 0)
        load_words(0)
        for q in range(4):
            nc.sync.dma_start(
                out=tab_s[32 * q : 32 * q + 8, :].bitcast(I32), in_=tab_scales[:, 4 * q : 4 * q + 4, :].bitcast(I32)
            )
        for a in range(2):
            nc.sync.dma_start(out=w1_raw[a][:], in_=w1[512 * a : 512 * (a + 1), :].rearrange("(p i) r -> p i r", i=4))
        for q in range(4):
            nc.sync.dma_start(
                out=w2_sraw[32 * q : 32 * q + 4, :].bitcast(I32), in_=w2_scales[0, 4 * q : 4 * q + 4, :].bitcast(I32)
            )
        load_words(1)
        nc.sync.dma_start(out=gain_t[:], in_=gain.rearrange("(p t) -> p t", t=4))
        nc.sync.dma_start(out=base_t[:], in_=base.rearrange("(p t) -> p t", t=4))
        nc.sync.dma_start(idx2[:], offs2)
        minus_base = held([P, 4], F32, "minus_base")
        nc.gpsimd.tensor_scalar(out=minus_base[:], in0=base_t[:], scalar1=-1.0, scalar2=0.0, op0=ALU.mult, op1=ALU.add)

        wgs_rows = wgs.rearrange("(q t) j -> q t j", t=4)
        page_rows = page0.rearrange("(p t) c -> p t c", t=4)

        def load_wgs(tag, start, count):
            tile = shared([P, 4, count], F32, tag)
            for q in (0, 2, 1, 3):
                nc.sync.dma_start(out=tile[32 * q : 32 * q + 32, :, :], in_=wgs_rows[:, :, start : start + count])
            return tile

        page = [shared([P, T2], F32, "page%d" % t) for t in range(4)]
        wg0 = load_wgs("wg0", 0, PIECE)
        for t in range(4):
            nc.sync.dma_start(out=page[t][:], in_=page_rows[:, t, :])
        wg1 = load_wgs("wg1", PIECE, PIECE)
        wg2 = load_wgs("wg2", 2 * PIECE, 2 * PIECE)
        nc.sync.dma_start(idx3[:], offs3)
        nc.sync.dma_start(out=vthr_t[:], in_=vthr.rearrange("(p t) -> p t", t=4))

        w2_c = held([P, 2 * H], U8, "w2_c")
        w2_s = held([P, H], U8, "w2_s")
        nc.vector.tensor_copy(
            out=w2_c[:].rearrange("p (t q b) -> p q t b", t=4, b=2), in_=w2_raw[:].rearrange("p (q t b) -> p q t b", t=4, b=2)
        )
        got_w0 = held([P, S], U32, "got_w0")
        nc.vector.tensor_copy(got_w0[:], tab_w[0][:].indirect(idx1[:]))
        got_s_first = held([P, PIECE], U8, "got_s_first")
        got_s_rest = held([P, S - PIECE], U8, "got_s_rest")
        nc.vector.tensor_copy(got_s_first[:], tab_s[:].indirect(entries(idx1, 0, PIECE)))
        nc.vector.tensor_copy(got_s_rest[:], tab_s[:].indirect(entries(idx1, PIECE, S - PIECE)))

        def deal_columns(engine_copy, grouped, raw, lo, hi):
            engine_copy(
                out=grouped[:].rearrange("p (t m i) -> p m i t", t=4, i=4)[:, lo:hi],
                in_=raw[:].rearrange("p i (m t) -> p m i t", t=4)[:, lo:hi],
            )

        w1_c = [held([P, H], U32, "w1_c%d" % a) for a in range(2)]
        w1_s = [held([P, H], U8, "w1_s%d" % a) for a in range(2)]
        w1_b = [shared([P, 4 * H], BF16, "wb%d" % a) for a in range(2)]
        deal_columns(nc.scalar.copy, w1_b[0], w1_raw[0], 0, 128)
        nc.vector.quantize_mx(out=w1_c[0][:].bitcast(E4M3), scales=w1_s[0][:], in_=w1_b[0][:])
        deal_columns(nc.scalar.copy, w1_b[1], w1_raw[1], 0, 64)
        deal_columns(nc.vector.tensor_copy, w1_b[1], w1_raw[1], 64, 128)
        nc.vector.quantize_mx(out=w1_c[1][:].bitcast(E4M3), scales=w1_s[1][:], in_=w1_b[1][:])

        def gather_words(out, start, count):
            nc.vector.tensor_copy(out, tab_w[1][:].indirect(entries(idx1, start, count)))

        got_w1 = {}

        def first_product(out, t, a, chunk, lo, width, start, stop):
            j0 = chunk + lo
            moving = got_w0[:, j0 : j0 + width] if a == 0 else got_w1[chunk][:, lo : lo + width]
            if chunk == 0:
                scales = got_s_first[4 * a : P, j0 : j0 + width]
            else:
                scales = got_s_rest[4 * a : P, j0 - PIECE : j0 - PIECE + width]
            nc.tensor.matmul_mx(
                out=out,
                lhsT=w1_c[a][:, P * t : P * (t + 1)].bitcast(E4M3),
                lhsT_scale=w1_s[a][:, P * t : P * (t + 1)],
                rhs=moving.bitcast(E4M3),
                rhs_scale=scales,
                start=start,
                stop=stop,
            )

        def second_product(out, t, codes, scales, start, stop):
            nc.tensor.matmul_mx(
                out=out,
                lhsT=w2_c[:, 2 * P * t : 2 * P * (t + 1)].bitcast(E2M1),
                lhsT_scale=w2_s[:, P * t : P * (t + 1)],
                rhs=codes.bitcast(E4M3),
                rhs_scale=scales,
                start=start,
                stop=stop,
            )

        def by_runs(rows):
            return rows.rearrange("p t (c i) -> p c t i", i=4)

        def side_by_side(grouped):
            return grouped.rearrange("p (c i t) -> p c t i", i=4, t=4)

        def interleave(engine_copy, grouped, rows):
            engine_copy(out=side_by_side(grouped), in_=by_runs(rows))

        def quantise(codes, scales, grouped):
            nc.vector.quantize_mx(out=codes.bitcast(E4M3), scales=scales, in_=grouped)

        def bend(zb):
            th = shared([P, BANK], F32, "th", 4)
            nc.scalar.activation(out=th[:], in_=zb[:], func=ACT.Tanh)
            return th

        def apply_gain(out, th, t):
            nc.scalar.activation(out=out, in_=th, func=ACT.Copy, scale=gain_t[:, t : t + 1])

        def add_z(out, pb, z):
            nc.vector.tensor_tensor(out=out, in0=pb, in1=z, op=ALU.add)

        def put(t, start, h, weights):
            nc.vector.tensor_tensor(page[t][:].indirect(entries(idx2, start, h.shape[1])), h, weights, ALU.mult)

        got_w1[0] = held([P, PIECE], U32, "got_w1_0")
        got_w1[PIECE] = held([P, PIECE], U32, "got_w1_1")
        for half in range(2):
            gather_words(got_w1[0][:, P * half : P * (half + 1)], P * half, P)
        gather_words(got_w1[PIECE][:], PIECE, PIECE)
        nc.vector.tensor_copy(
            out=w2_s[:].rearrange("p (t q) -> p q t", t=4), in_=w2_sraw[:].rearrange("p (q t) -> p q t", t=4)
        )
        z_banks = [bank("z"), bank("z")]
        for a in range(2):
            for half in range(2):
                for t in range(4):
                    first_product(
                        z_banks[half][:, P * t : P * (t + 1)], t, a, 0, P * half, P,
                        start=(a == 0 and t == 0), stop=(a == 1 and t == 3),
                    )
        bent = []
        for half in range(2):
            th = shared([P, BANK], F32, "th", 4)
            nc.scalar.activation(
                out=th[:].rearrange("p (j t) -> p j t", t=4),
                in_=z_banks[half][:].rearrange("p (t j) -> p j t", t=4),
                func=ACT.Tanh,
            )
            bent.append(th)
        f_half = [shared([P, 4 * P], BF16, "f_half%d" % half) for half in range(2)]
        f_c0 = [held([P, P], U32, "f_c0_%d" % half) for half in range(2)]
        f_s0 = [held([P, P], U8, "f_s0_%d" % half) for half in range(2)]
        for half in range(2):
            nc.vector.tensor_tensor(
                out=f_half[half][:].rearrange("p (j t) -> p j t", t=4),
                in0=bent[half][:].rearrange("p (j t) -> p j t", t=4),
                in1=gain_t[:].unsqueeze(1).to_broadcast([P, P, 4]),
                op=ALU.mult,
            )
        for half in range(2):
            quantise(f_c0[half][:], f_s0[half][:], f_half[half][:])
        h_banks = [bank("mix"), bank("mix")]
        for pair in range(2):
            for a in range(2):
                for u in range(2):
                    first_product(
                        h_banks[pair][:, PIECE * u : PIECE * (u + 1)], 2 * pair + u, a, 0, 0, PIECE,
                        start=(u == 0 and a == 0), stop=False,
                    )
        for half in range(2):
            for pair in range(2):
                for u in range(2):
                    col = PIECE * u + P * half
                    second_product(
                        h_banks[pair][:, col : col + P], 2 * pair + u, f_c0[half][:], f_s0[half][:],
                        start=False, stop=(half == 1 and u == 1),
                    )

        def empty_h(t, tag):
            h = shared([P, PIECE], F32, tag)
            nc.scalar.copy(out=h[:], in_=h_banks[t // 2][:, PIECE * (t % 2) : PIECE * (t % 2 + 1)])
            return h

        h0 = [empty_h(t, "h0%d" % t) for t in range(3)]
        got_w1[2 * PIECE] = shared([P, 2 * PIECE], U32, "f_half1")
        gather_words(got_w1[2 * PIECE][:], 2 * PIECE, 2 * PIECE)

        f_rows1 = shared([P, 4, PIECE], BF16, "f_rows1")
        z1_banks = []
        for pair in range(2):
            zb = bank("z")
            for u in range(2):
                for a in range(2):
                    first_product(
                        zb[:, PIECE * u : PIECE * (u + 1)], 2 * pair + u, a, PIECE, 0, PIECE, start=(a == 0), stop=(a == 1)
                    )
            th = bend(zb)
            for u in range(2):
                apply_gain(f_rows1[:, 2 * pair + u, :], th[:, PIECE * u : PIECE * (u + 1)], 2 * pair + u)
            z1_banks.append(zb)
        f_b1 = held([P, 4 * PIECE], BF16, "f_b1")
        interleave(nc.scalar.copy, f_b1[:], f_rows1[:])
        h0.append(empty_h(3, "f_rows1"))
        z1 = [held([P, BANK], F32, "z1_%d" % pair) for pair in range(2)]
        for pair in range(2):
            nc.scalar.copy(out=z1[pair][:], in_=z1_banks[pair][:])

        f_rows2 = shared([P, 4, BANK], BF16, "wb0")
        z2_banks = []
        for t in range(4):
            zb = bank("z")
            for a in range(2):
                first_product(zb[:], t, a, 2 * PIECE, 0, BANK, start=(a == 0), stop=(a == 1))
            apply_gain(f_rows2[:, t, :], bend(zb)[:], t)
            z2_banks.append(zb)
        f_b2 = shared([P, 4 * BANK], BF16, "wb1")
        interleave(nc.scalar.copy, f_b2[:], f_rows2[:])
        z2 = [held([P, BANK], F32, "z2_%d" % t) for t in range(4)]
        for t in range(4):
            nc.scalar.copy(out=z2[t][:], in_=z2_banks[t][:])

        w3_raw = [shared([P, 4, BANK], F32, "slab%d" % g) for g in range(2)]
        for g in range(2):
            nc.sync.dma_start(out=w3_raw[g][:], in_=w3.rearrange("(p i) n -> p i n", i=4)[:, :, 512 * g : 512 * (g + 1)])
        view_t = held([P, 4, PW], F32, "view_t")
        nc.sync.dma_start(out=view_t[:], in_=view.rearrange("(p t) j -> p t j", t=4))
        w3_b = [shared([P, 4 * BANK], BF16, "wb0")]
        deal_columns(nc.scalar.copy, w3_b[0], w3_raw[0], 0, 128)

        for t in range(3):
            put(t, 0, h0[t][:], wg0[:, t, :])
        f_c1 = shared([P, PIECE], U32, "h01")
        f_s1 = held([P, PIECE], U8, "f_s1")
        quantise(f_c1[:], f_s1[:], f_b1[:])
        mix1 = [bank("mix"), bank("mix")]
        for t in range(4):
            col = PIECE * (t % 2)
            second_product(mix1[t // 2][:, col : col + PIECE], t, f_c1[:], f_s1[:], start=True, stop=True)
        put(3, 0, h0[3][:], wg0[:, 3, :])
        h1_pair = shared([P, BANK], F32, "h1_pair")
        h12 = held([P, PIECE], F32, "h12")
        add_z(h1_pair[:], mix1[0][:], z1[0][:])
        add_z(h12[:], mix1[1][:, 0:PIECE], z1[1][:, 0:PIECE])
        for t in range(2):
            put(t, PIECE, h1_pair[:, PIECE * t : PIECE * (t + 1)], wg1[:, t, :])
        put(2, PIECE, h12[:], wg1[:, 2, :])
        f_c2 = shared([P, BANK], U32, "h1_pair")
        f_s2 = held([P, BANK], U8, "f_s2")
        quantise(f_c2[:], f_s2[:], f_b2[:])
        h13 = shared([P, PIECE], F32, "wb1")
        add_z(h13[:], mix1[1][:, PIECE:BANK], z1[1][:, PIECE:BANK])
        put(3, PIECE, h13[:], wg1[:, 3, :])
        w3_b.append(shared([P, 4 * BANK], BF16, "wb1"))
        deal_columns(nc.scalar.copy, w3_b[1], w3_raw[1], 0, 128)

        mix2 = []
        for t in range(4):
            pb = bank("mix")
            second_product(pb[:], t, f_c2[:], f_s2[:], start=True, stop=True)
            mix2.append(pb)

        centred = held([P, 4, PW], F32, "centred")

        def look(t, start, count, tag):
            seen = shared([P, count], F32, tag)
            nc.scalar.activation(
                out=seen[:], in_=page[t][:].indirect(entries(idx3, start, count)), func=ACT.Sigmoid, bias=vthr_t[:, t : t + 1]
            )
            return seen

        def centre(t, start, seen):
            nc.scalar.activation(
                out=centred[:, t, start : start + seen.shape[1]], in_=seen, func=ACT.Identity, bias=minus_base[:, t : t + 1]
            )

        h2 = {}

        def add_last(t):
            h2[t] = shared([P, BANK], F32, "h2_%d" % (t % 2))
            add_z(h2[t][:], mix2[t][:], z2[t][:])

        def put_last(t):
            put(t, 2 * PIECE, h2[t][:], wg2[:, t, :])

        add_last(0)
        add_last(1)
        put_last(0)
        centre(0, 0, look(0, 0, PW, "slab1")[:])
        add_last(2)
        put_last(1)
        centre(1, 0, look(1, 0, PW, "page0")[:])
        add_last(3)
        put_last(2)
        seen2 = look(2, 0, PW, "page1")
        centre(2, 0, seen2[:, 0:BANK])
        put_last(3)
        w3_c = [shared([P, BANK], U32, ("h2_1", "wg2")[g]) for g in range(2)]
        w3_s = [held([P, BANK], U8, "w3_s%d" % g) for g in range(2)]
        for g in range(2):
            quantise(w3_c[g][:], w3_s[g][:], w3_b[g][:])
        nc.vector.tensor_scalar(
            out=centred[:, 2, BANK:PW], in0=seen2[:, BANK:PW], scalar1=base_t[:, 2:3], scalar2=None, op0=ALU.subtract
        )
        for half in range(2):
            centre(3, BANK * half, look(3, BANK * half, BANK, "page2")[:])

        starts = (0, P, PIECE, BANK)
        widths = (P, P, PIECE, BANK)
        d_b = [held([P, 4 * w], BF16, "d_b%d" % n) for n, w in enumerate(widths)]
        d_c = [held([P, w], U32, "d_c%d" % n) for n, w in enumerate(widths)]
        d_s = [held([P, w], U8, "d_s%d" % n) for n, w in enumerate(widths)]

        def weigh(n, lo, count):
            cols = slice(starts[n] + lo, starts[n] + lo + count)
            nc.vector.tensor_tensor(
                out=side_by_side(d_b[n][:, 4 * lo : 4 * (lo + count)]),
                in0=by_runs(centred[:, :, cols]),
                in1=by_runs(view_t[:, :, cols]),
                op=ALU.mult,
            )

        def quantise_d(n):
            quantise(d_c[n][:], d_s[n][:], d_b[n][:])

        weigh(0, 0, P)
        weigh(1, 0, P)
        quantise_d(0)
        quantise_d(1)
        weigh(2, 0, PIECE)
        weigh(3, 0, PIECE)
        quantise_d(2)
        weigh(3, PIECE, PIECE)
        quantise_d(3)

        y = {}
        for half in range(2):
            for g in range(2):
                y[g, half] = shared([P, 4, BANK], F32, (("slab0", "slab1"), ("page2", "page3"))[half][g])
        y_c = {key: held([P, BANK], U32, "y_c%d%d" % key) for key in y}
        y_s = [held([P, BANK], U8, "y_s%d" % half) for half in range(2)]
        out_rows = out_0.rearrange("(g p t) j -> g p t j", g=2, t=4)

        def third_product(g, n, first, count, tag):
            width = widths[n]
            half, lo = divmod(starts[n], BANK)
            yb = bank(tag)
            for u in range(count):
                t = first + u
                nc.tensor.matmul_mx(
                    out=yb[:, width * u : width * (u + 1)],
                    lhsT=w3_c[g][:, P * t : P * (t + 1)].bitcast(E4M3),
                    lhsT_scale=w3_s[g][:, P * t : P * (t + 1)],
                    rhs=d_c[n][:].bitcast(E4M3),
                    rhs_scale=d_s[n][:],
                    start=True,
                    stop=True,
                )
            nc.scalar.copy(
                out=y[g, half][:, first : first + count, lo : lo + width], in_=yb[:].rearrange("p (u j) -> p u j", u=count)
            )

        def store_y(g, half, rows, lo, count):
            nc.sync.dma_start(
                out=out_rows[g][:, rows, BANK * half + lo : BANK * half + lo + count], in_=y[g, half][:, rows, lo : lo + count]
            )

        for g in range(2):
            for n in range(2):
                third_product(g, n, 0, 4, ("z", "mix")[n])
            store_y(g, 0, slice(0, 4), 0, PIECE)
        for g in range(2):
            for pair in range(2):
                third_product(g, 2, 2 * pair, 2, ("z", "mix")[pair])
            store_y(g, 0, slice(0, 4), PIECE, PIECE)
        for g in range(2):
            for t in range(4):
                third_product(g, 3, t, 1, ("z", "mix")[t % 2])
                if t % 2 == 1:
                    store_y(g, 1, slice(t - 1, t + 1), 0, BANK)

        order = [(g, 0, lo) for lo in (0, PIECE) for g in range(2)] + [(g, 1, lo) for g in range(2) for lo in (0, PIECE)]

        def group_y(k):
            g, half, lo = order[k]
            y_b = shared([P, 4 * PIECE], BF16, "y_b", 3)
            engine_copy = nc.scalar.copy if k == len(order) - 1 else nc.vector.tensor_copy
            interleave(engine_copy, y_b[:], y[g, half][:, :, lo : lo + PIECE])
            return y_b

        grouped = group_y(0)
        for k, (g, half, lo) in enumerate(order):
            current = grouped
            if k + 1 < len(order):
                grouped = group_y(k + 1)
            quantise(y_c[g, half][:, lo : lo + PIECE], y_s[half][4 * g : P, lo : lo + PIECE], current[:])
            if lo == PIECE:
                nc.sync.dma_start(
                    out=out_1[g].rearrange("p j i -> p (j i)").bitcast(I32)[:, BANK * half : BANK * (half + 1)],
                    in_=y_c[g, half][:].bitcast(I32),
                )
                if g == 1:
                    for q in range(4):
                        queue = nc.scalar if half == 1 and q % 2 == 1 else nc.sync
                        queue.dma_start(
                            out=out_2[:, 4 * q : 4 * q + 4, BANK * half : BANK * (half + 1)].bitcast(I32),
                            in_=y_s[half][32 * q : 32 * q + 8, :].bitcast(I32),
                        )
